import numpy as np
import ml_dtypes


def mxq(x, axis, fmt="e4m3"):
    dtype, down = {"e4m3": (ml_dtypes.float8_e4m3fn, 7), "e5m2": (ml_dtypes.float8_e5m2, 14)}[fmt]
    v = np.moveaxis(np.asarray(x, np.float32).astype(ml_dtypes.bfloat16).astype(np.float64), axis, -1)
    blocks = v.reshape(v.shape[:-1] + (-1, 32))
    amax = np.abs(blocks).max(-1, keepdims=True)
    byte = np.maximum(np.where(amax > 0, np.frexp(amax)[1] - 1 + 127, 0) - down, 1)
    scale = np.exp2(byte - 127.0)
    codes = (blocks / scale).astype(np.float32).astype(dtype).astype(np.float64)
    return np.moveaxis((codes * scale).reshape(v.shape), -1, axis)


WIDE = False


def mx_kscale(k):
    if not WIDE:
        return np.ones(k)
    levels = np.array([30, -30])
    if k % 512:
        return np.exp2(np.random.permutation(np.resize(levels, k // 32))).repeat(32)
    a = np.empty((k // 512, 16))
    for p in range(k // 512):
        a[p, :8] = np.random.permutation(np.resize(levels, 8))
        for g in range(8):
            far = levels[np.abs(levels - a[p, g]) >= 10]
            a[p, g + 8] = far[np.random.randint(len(far))]
    return np.exp2(a.ravel()).repeat(32)


def f64(x):
    return np.asarray(x).astype(np.float64)


def striped(idx):
    return np.tile(np.asarray(idx).reshape(-1, 16).T, (8, 1)).astype(np.uint16)


def unstriped(offs):
    return offs[:16].T.reshape(-1).astype(np.int64)


E2M1 = np.array([0.0, 0.5, 1.0, 1.5, 2.0, 3.0, 4.0, 6.0, -0.0, -0.5, -1.0, -1.5, -2.0, -3.0, -4.0, -6.0])


def pack_weight(w, fmt):
    k, n = w.shape
    w = f64(np.asarray(w, np.float32).astype(ml_dtypes.bfloat16)).reshape(k // 32, 32, n)
    amax = np.abs(w).max(1)
    if fmt in ("e4m3", "e5m2"):
        byte = np.frexp(amax)[1] - 1 + 127 - (7 if fmt == "e4m3" else 14)
    else:
        mant, ex = np.frexp(amax / 6.0)
        byte = np.where(mant > 0.5, ex, ex - 1) + 127
    byte = np.clip(np.where(amax > 0, byte, 1), 1, 254)
    scaled = (w * np.exp2(127.0 - byte)[:, None, :]).reshape(k, n).astype(np.float32)
    by_word = np.ascontiguousarray(scaled.reshape(k // 512, 128, 4, n).transpose(0, 1, 3, 2))
    if fmt in ("e4m3", "e5m2"):
        words = by_word.astype(ml_dtypes.float8_e4m3fn if fmt == "e4m3" else ml_dtypes.float8_e5m2).view(np.uint8)
    else:
        c = by_word.astype(ml_dtypes.float4_e2m1fn).view(np.uint8) & 0xF
        words = (c[..., 0::2] | (c[..., 1::2] << 4)).reshape(k // 512, 128, 2 * n)
    return np.ascontiguousarray(words), np.ascontiguousarray(byte.astype(np.uint8).reshape(k // 512, 16, n))


def unpack_weight(words, scales, fmt):
    g, _, n = scales.shape
    words = np.ascontiguousarray(words).reshape(g, 128, n, -1)
    if fmt in ("e4m3", "e5m2"):
        vals = words.view(ml_dtypes.float8_e4m3fn if fmt == "e4m3" else ml_dtypes.float8_e5m2).astype(np.float64)
    else:
        nib = np.empty((g, 128, n, 4), np.uint8)
        nib[..., 0::2] = words & 0xF
        nib[..., 1::2] = words >> 4
        vals = E2M1[nib]
    vals = vals * np.repeat(np.exp2(scales.astype(np.float64) - 127.0), 8, axis=1)[..., None]
    return vals.transpose(0, 1, 3, 2).reshape(g * 512, n)


def sigmoid(v):
    return 1.0 / (1.0 + np.exp(-v))


def sgn(shape):
    return np.random.uniform(0.5, 2.0, shape) * np.where(np.random.standard_normal(shape) < 0, -1.0, 1.0)


K, T, J, R, V, N, O = 512, 1024, 256, 512, 1024, 256, 128


def setup_inputs():
    n = np.random.standard_normal
    idx = np.random.permutation(V)[:R]
    idx2 = np.random.permutation(T)[:J]
    idx3 = np.random.permutation(J)[:O]
    idx4 = np.random.permutation(J)[:O]
    idx5 = np.random.permutation(J)[:O]
    idx6 = np.random.permutation(J)[:O]
    fk = mx_kscale(K)
    fr = mx_kscale(R)
    tr = np.ones(V)
    tr[idx] = fr
    xtp = pack_weight(n((K, T)) / fk[:, None], "e2m1")
    wtp = pack_weight(n((K, V)) * 1 / np.sqrt(K) * fk[:, None] * tr, "e4m3")
    w2p = pack_weight(n((K, R)) * 1 / np.sqrt(K) * fk[:, None] * fr, "e5m2")
    wbp = pack_weight(n((R, N)) * 1 / np.sqrt(R) / fr[:, None], "e2m1")
    wcp = pack_weight(n((R, N)) * 1 / np.sqrt(R) / fr[:, None], "e5m2")
    return {
        "xt_words": xtp[0],
        "xt_scales": xtp[1],
        "wt_words": wtp[0],
        "wt_scales": wtp[1],
        "w2_words": w2p[0],
        "w2_scales": w2p[1],
        "wb_words": wbp[0],
        "wb_scales": wbp[1],
        "wc_words": wcp[0],
        "wc_scales": wcp[1],
        "so": (np.random.uniform(0.5, 1.6, (N, 1))).astype(np.float32),
        "sp": (sgn((N, 1))).astype(np.float32),
        "bo": (np.random.uniform(-2.0, 2.0, (N, 1))).astype(np.float32),
        "so2": (np.random.uniform(0.5, 1.6, (N, 1))).astype(np.float32),
        "sp2": (sgn((N, 1))).astype(np.float32),
        "bo2": (np.random.uniform(-2.0, 2.0, (N, 1))).astype(np.float32),
        "offs": striped(idx),
        "offs2": striped(idx2),
        "offs3": striped(idx3),
        "offs4": striped(idx4),
        "offs5": striped(idx5),
        "offs6": striped(idx6),
    }


def reference(xt_words, xt_scales, wt_words, wt_scales, w2_words, w2_scales, wb_words, wb_scales, wc_words, wc_scales, so, sp, bo, so2, sp2, bo2, offs, offs2, offs3, offs4, offs5, offs6):
    idx = unstriped(offs)
    idx2 = unstriped(offs2)
    idx3 = unstriped(offs3)
    idx4 = unstriped(offs4)
    idx5 = unstriped(offs5)
    idx6 = unstriped(offs6)
    xtu = unpack_weight(xt_words, xt_scales, "e2m1")
    wtu = unpack_weight(wt_words, wt_scales, "e4m3")
    w2u = unpack_weight(w2_words, w2_scales, "e5m2")
    wbu = unpack_weight(wb_words, wb_scales, "e2m1")
    wcu = unpack_weight(wc_words, wc_scales, "e5m2")
    wtidxg = wtu[:, idx]
    xtidx2g = xtu[:, idx2]
    a = wtidxg.T @ xtidx2g
    b = w2u.T @ xtidx2g
    hid = np.abs(a - b)
    hidq = mxq(hid, 0, "e5m2")
    p = wbu.T @ hidq
    q = wcu.T @ hidq
    y = p[:, idx3] * f64(so) * sigmoid(q[:, idx4] * f64(sp) + f64(bo)) - q[:, idx5] * f64(so2) * sigmoid(p[:, idx6] * f64(sp2) + f64(bo2))
    return y

@@ -1,0 +1,208 @@
+from contextlib import ExitStack
+
+import concourse.mybir as mybir
+
+K, T, J, R, V, N, O = 512, 1024, 256, 512, 1024, 256, 128
+FLOPS = 2 * (2 * K * R * J + 2 * R * N * J)
+
+F32 = mybir.dt.float32
+BF16 = mybir.dt.bfloat16
+I32 = mybir.dt.int32
+U32 = mybir.dt.uint32
+U16 = mybir.dt.uint16
+U8 = mybir.dt.uint8
+E4M3 = mybir.dt.float8_e4m3fn_x4
+E5M2 = mybir.dt.float8_e5m2_x4
+E2M1 = mybir.dt.float4_e2m1fn_x4
+ACT = mybir.ActivationFunctionType
+ALU = mybir.AluOpType
+
+P = 128
+PACK = 4
+QUADS = 4
+HALF = J // 2
+PAD = 8
+
+
+def tile_list_outcomegatedcross_storeleads_kernel(
+    tc, xt_words, xt_scales, wt_words, wt_scales, w2_words, w2_scales, wb_words, wb_scales,
+    wc_words, wc_scales, so, sp, bo, so2, sp2, bo2, offs, offs2, offs3, offs4, offs5, offs6, out,
+):
+    nc = tc.nc
+    with ExitStack() as ctx:
+        sb = ctx.enter_context(tc.tile_pool(name="sb", bufs=1))
+        psum = ctx.enter_context(tc.psum_pool(name="psum", bufs=1))
+
+        def sbt(name, shape, dtype):
+            return sb.tile(shape, dtype, name=name, align_bytes=64)
+
+        def load_list(name, src):
+            lst = sb.tile(list(src.shape), U16, name=name)
+            nc.sync.dma_start(lst[:], src)
+            return lst
+
+        def load_scale_rows(queue, plane, src, quads):
+            for q in quads:
+                queue.dma_start(
+                    plane[32 * q : 32 * q + 4, :].bitcast(I32),
+                    src[0, 4 * q : 4 * q + 4, :].bitcast(I32),
+                )
+
+        wt_s = sbt("wt_s", [P, V], U8)
+        xt_s = sbt("xt_s", [P, T], U8)
+        w2_s = sbt("w2_s", [P, R], U8)
+        wo_stage = sbt("wo_stage", [P // 2, 2, 2 * N], U8)
+        wo_s = sbt("wo_s", [P, 2 * N], U8)
+        nc.vector.memset(w2_s[:].bitcast(I32), 0)
+        nc.vector.memset(wt_s[:].bitcast(I32), 0)
+        nc.vector.memset(wo_stage[:].bitcast(I32), 0)
+
+        def load_scale_quadrant(queue, plane, src, q):
+            rows = src[0, 4 * q : 4 * q + 4, :].bitcast(I32)
+            queue.dma_start(
+                plane[32 * q : 32 * (q + 1), :].bitcast(I32),
+                rows.unsqueeze(0).broadcast_to([8, 4, rows.shape[1]]),
+            )
+
+        w2_w = sbt("w2_w", [P, R], U32)
+        nc.gpsimd.dma_start(w2_w[:].bitcast(I32), w2_words[0].rearrange("p n t -> p (n t)").bitcast(I32))
+        xt_w = sbt("xt_w", [P, T], U16)
+        nc.sync.dma_start(xt_w[:].bitcast(I32), xt_words[0].bitcast(I32))
+        for q in range(3):
+            load_scale_quadrant(nc.scalar, xt_s, xt_scales, q)
+        l2 = load_list("l2", offs2)
+        l1 = load_list("l1", offs)
+        load_scale_quadrant(nc.sync, xt_s, xt_scales, 3)
+        wt_w = sbt("wt_w", [P, V], U32)
+        nc.sync.dma_start(wt_w[:].bitcast(I32), wt_words[0].rearrange("p n t -> p (n t)").bitcast(I32))
+        load_scale_rows(nc.sync, w2_s, w2_scales, range(QUADS))
+        load_scale_rows(nc.sync, wt_s, wt_scales, (0, 1, 2))
+        load_scale_rows(nc.gpsimd, wt_s, wt_scales, (3,))
+
+        for i, src in enumerate((wb_scales, wc_scales)):
+            by_pair = src[0].bitcast(I32).rearrange("(u q r) c -> q r u c", u=2, r=4)
+            for q in range(2):
+                nc.sync.dma_start(wo_stage[32 * q : 32 * q + 4, :, i * N : (i + 1) * N].bitcast(I32), by_pair[q])
+        wb_w = sbt("wb_w", [P, N], U16)
+        nc.sync.dma_start(wb_w[:].bitcast(I32), wb_words[0].bitcast(I32))
+        wc_w = sbt("wc_w", [P, N], U32)
+        nc.sync.dma_start(wc_w[:].bitcast(I32), wc_words[0].rearrange("p n t -> p (n t)").bitcast(I32))
+        l6 = load_list("l6", offs6)
+        l3 = load_list("l3", offs3)
+        l4 = load_list("l4", offs4)
+        l5 = load_list("l5", offs5)
+        cols = {}
+        with nc.allow_non_contiguous_dma(reason="one value a partition"):
+            for name, src in (("sp2", sp2), ("bo2", bo2), ("so", so), ("sp", sp), ("bo", bo), ("so2", so2)):
+                col = sb.tile([P, 2, PAD], F32, name="col_" + name)
+                nc.sync.dma_start(col[:, :, 0:1], src.rearrange("(h p) o -> p h o", p=P))
+                cols[name] = col
+
+        xg_w = sbt("xg_w", [P, J], U16)
+        nc.vector.tensor_copy(xg_w[:], xt_w[:].indirect(l2[:]))
+        xg_s = sbt("xg_s", [P, J], U8)
+        nc.vector.tensor_copy(xg_s[:], xt_s[:].indirect(l2[:]))
+        wg_w = sbt("wg_w", [P, R], U32)
+        nc.vector.tensor_copy(wg_w[:].rearrange("p (t m) -> p m t", t=PACK), wt_w[:].indirect(l1[:]))
+        wg_s = sbt("wg_s", [P, R], U8)
+        nc.vector.tensor_copy(wg_s[:].rearrange("p (t m) -> p m t", t=PACK), wt_s[:].indirect(l1[:]))
+
+        w2d_w = sbt("w2d_w", [P, R], U32)
+        nc.scalar.copy(w2d_w[:].rearrange("p (t m) -> p m t", t=PACK), w2_w[:].rearrange("p (m t) -> p m t", t=PACK))
+        w2d_s = sbt("w2d_s", [P, R], U8)
+        for t in range(PACK):
+            nc.gpsimd.tensor_copy(w2d_s[:, t * P : (t + 1) * P], w2_s[:, t::PACK])
+
+        def first_stage(bank, words, scales, fmt, h, t):
+            slots = slice(h * HALF, (h + 1) * HALF)
+            feats = slice(t * P, (t + 1) * P)
+            nc.tensor.matmul_mx(
+                out=bank[:, t, :],
+                lhsT=words[:, feats].bitcast(fmt),
+                lhsT_scale=scales[:, feats],
+                rhs=xg_w[:, slots].bitcast(E2M1),
+                rhs_scale=xg_s[:, slots],
+                start=True,
+                stop=True,
+            )
+
+        b_banks = [psum.tile([P, PACK, HALF], F32, name="b_bank%d" % h) for h in range(2)]
+        a_banks = [psum.tile([P, PACK, HALF], F32, name="a_bank%d" % h) for h in range(2)]
+        for t in range(PACK):
+            for h in range(2):
+                first_stage(b_banks[h], w2d_w, w2d_s, E5M2, h, t)
+        b_sb = []
+        for h in range(2):
+            b_half = sbt("b_sb%d" % h, [P, HALF, PACK], F32)
+            nc.scalar.activation(b_half[:], b_banks[h][:].rearrange("p t j -> p j t"), ACT.Copy)
+            b_sb.append(b_half)
+        for h in range(2):
+            for t in range(PACK):
+                first_stage(a_banks[h], wg_w, wg_s, E4M3, h, t)
+
+        for u in range(2):
+            nc.vector.tensor_copy(wo_s[64 * u : 64 * (u + 1), :].bitcast(I32), wo_stage[:, u, :].bitcast(I32))
+
+        hid = []
+        for h in range(2):
+            hid_half = sbt("hid%d" % h, [P, HALF, PACK], BF16)
+            for c in range(2):
+                part = slice(c * HALF // 2, (c + 1) * HALF // 2)
+                diff = sbt("diff%d%d" % (h, c), [P, HALF // 2, PACK], F32)
+                a_part = a_banks[h][:].rearrange("p t j -> p j t")[:, part, :]
+                nc.vector.tensor_tensor(diff[:], a_part, b_sb[h][:, part, :], ALU.subtract)
+                nc.scalar.activation(hid_half[:, part, :], diff[:], ACT.Abs)
+            hid.append(hid_half)
+
+        rows = {}
+        for which in ("p", "q"):
+            for g in range(2):
+                rows[which, g] = sbt("%s_rows%d" % (which, g), [P, J], F32)
+        second = {"p": (wb_w, E2M1, 0), "q": (wc_w, E5M2, N)}
+        order = [("p", 0), ("q", 0), ("p", 1), ("q", 1)]
+        for h in range(2):
+            hq_w = sbt("hq_w%d" % h, [P, HALF], U32)
+            hq_s = sbt("hq_s%d" % h, [P, HALF], U8)
+            nc.vector.quantize_mx(out=hq_w[:].bitcast(E5M2), scales=hq_s[:], in_=hid[h][:].rearrange("p j t -> p (j t)"))
+            if h == 0:
+                shared = psum.tile([P, 4, HALF], F32, name="o_bank0")
+                places = [shared[:, i, :] for i in range(4)]
+            else:
+                lone_p = psum.tile([P, HALF], F32, name="o_bank1")
+                lone_q = psum.tile([P, HALF], F32, name="o_bank2")
+                shared = psum.tile([P, 2, HALF], F32, name="o_bank3")
+                places = [lone_p[:], lone_q[:], shared[:, 0, :], shared[:, 1, :]]
+            for (which, g), place in zip(order, places):
+                words, fmt, s0 = second[which]
+                nc.tensor.matmul_mx(
+                    out=place,
+                    lhsT=words[:, g * P : (g + 1) * P].bitcast(fmt),
+                    lhsT_scale=wo_s[:, s0 + g * P : s0 + (g + 1) * P],
+                    rhs=hq_w[:].bitcast(E5M2),
+                    rhs_scale=hq_s[:],
+                    start=True,
+                    stop=True,
+                )
+            for key, place in zip(order, places):
+                nc.vector.tensor_copy(rows[key][:, h * HALF : (h + 1) * HALF], place)
+
+        for g in range(2):
+            def col(name):
+                return cols[name][:, g, 0:1]
+
+            p_rows, q_rows = rows["p", g], rows["q", g]
+            gate_q = sbt("gate_q%d" % g, [P, O], F32)
+            nc.scalar.activation(gate_q[:], p_rows[:].indirect(l6[:]), ACT.Sigmoid, bias=col("bo2"), scale=col("sp2"))
+            p_pick = sbt("p_pick%d" % g, [P, O], F32)
+            nc.scalar.activation(p_pick[:], p_rows[:].indirect(l3[:]), ACT.Copy, scale=col("so"))
+            gate_p = sbt("gate_p%d" % g, [P, O], F32)
+            nc.scalar.activation(gate_p[:], q_rows[:].indirect(l4[:]), ACT.Sigmoid, bias=col("bo"), scale=col("sp"))
+            q_pick = sbt("q_pick%d" % g, [P, O], F32)
+            nc.scalar.activation(q_pick[:], q_rows[:].indirect(l5[:]), ACT.Copy, scale=col("so2"))
+            first = sbt("first%d" % g, [P, O], F32)
+            nc.vector.tensor_tensor(first[:], p_pick[:], gate_p[:], ALU.mult)
+            other = sbt("other%d" % g, [P, O], F32)
+            nc.vector.tensor_tensor(other[:], q_pick[:], gate_q[:], ALU.mult)
+            result = sbt("result%d" % g, [P, O], F32)
+            nc.vector.tensor_tensor(result[:], first[:], other[:], ALU.subtract)
+            nc.sync.dma_start(out[g * P : (g + 1) * P, :], result[:])

@@ -20,8 +20,16 @@ ALU = mybir.AluOpType
 P = 128
 PACK = 4
 QUADS = 4
-HALF = J // 2
+QUAD = P // QUADS
+LIVE = 4
+HALVES = 2
+HALF = J // HALVES
+PARTS = 2
+PART = HALF // PARTS
+DEAL = 2
+GROUPS = N // P
 PAD = 8
+ALIGN = 64
 
 
 def tile_list_outcomegatedcross_storeleads_kernel(
@@ -33,176 +41,204 @@ def tile_list_outcomegatedcross_storeleads_kernel(
         sb = ctx.enter_context(tc.tile_pool(name="sb", bufs=1))
         psum = ctx.enter_context(tc.psum_pool(name="psum", bufs=1))
 
-        def sbt(name, shape, dtype):
-            return sb.tile(shape, dtype, name=name, align_bytes=64)
+        def sb_tile(name, shape, dtype):
+            return sb.tile(shape, dtype, name=name, align_bytes=ALIGN)
 
         def load_list(name, src):
-            lst = sb.tile(list(src.shape), U16, name=name)
-            nc.sync.dma_start(lst[:], src)
-            return lst
+            offsets = sb.tile(list(src.shape), U16, name=name)
+            nc.sync.dma_start(offsets[:], src)
+            return offsets
 
-        def load_scale_rows(queue, plane, src, quads):
-            for q in quads:
+        def load_words(queue, name, src, columns, dtype):
+            words = sb_tile(name, [P, columns], dtype)
+            queue.dma_start(words[:].bitcast(I32), src.bitcast(I32))
+            return words
+
+        def fp8_rows(src):
+            return src[0].rearrange("p n t -> p (n t)")
+
+        def load_live_rows(queue, plane, src, quadrants):
+            for quad in quadrants:
                 queue.dma_start(
-                    plane[32 * q : 32 * q + 4, :].bitcast(I32),
-                    src[0, 4 * q : 4 * q + 4, :].bitcast(I32),
+                    plane[QUAD * quad : QUAD * quad + LIVE, :].bitcast(I32),
+                    src[0, LIVE * quad : LIVE * (quad + 1), :].bitcast(I32),
                 )
 
-        wt_s = sbt("wt_s", [P, V], U8)
-        xt_s = sbt("xt_s", [P, T], U8)
-        w2_s = sbt("w2_s", [P, R], U8)
-        wo_stage = sbt("wo_stage", [P // 2, 2, 2 * N], U8)
-        wo_s = sbt("wo_s", [P, 2 * N], U8)
-        nc.vector.memset(w2_s[:].bitcast(I32), 0)
-        nc.vector.memset(wt_s[:].bitcast(I32), 0)
-        nc.vector.memset(wo_stage[:].bitcast(I32), 0)
-
-        def load_scale_quadrant(queue, plane, src, q):
-            rows = src[0, 4 * q : 4 * q + 4, :].bitcast(I32)
+        def load_filled_quadrant(queue, plane, src, quad):
+            rows = src[0, LIVE * quad : LIVE * (quad + 1), :].bitcast(I32)
             queue.dma_start(
-                plane[32 * q : 32 * (q + 1), :].bitcast(I32),
-                rows.unsqueeze(0).broadcast_to([8, 4, rows.shape[1]]),
+                plane[QUAD * quad : QUAD * (quad + 1), :].bitcast(I32),
+                rows.unsqueeze(0).broadcast_to([QUAD // LIVE, LIVE, rows.shape[1]]),
             )
 
-        w2_w = sbt("w2_w", [P, R], U32)
-        nc.gpsimd.dma_start(w2_w[:].bitcast(I32), w2_words[0].rearrange("p n t -> p (n t)").bitcast(I32))
-        xt_w = sbt("xt_w", [P, T], U16)
-        nc.sync.dma_start(xt_w[:].bitcast(I32), xt_words[0].bitcast(I32))
-        for q in range(3):
-            load_scale_quadrant(nc.scalar, xt_s, xt_scales, q)
-        l2 = load_list("l2", offs2)
-        l1 = load_list("l1", offs)
-        load_scale_quadrant(nc.sync, xt_s, xt_scales, 3)
-        wt_w = sbt("wt_w", [P, V], U32)
-        nc.sync.dma_start(wt_w[:].bitcast(I32), wt_words[0].rearrange("p n t -> p (n t)").bitcast(I32))
-        load_scale_rows(nc.sync, w2_s, w2_scales, range(QUADS))
-        load_scale_rows(nc.sync, wt_s, wt_scales, (0, 1, 2))
-        load_scale_rows(nc.gpsimd, wt_s, wt_scales, (3,))
+        def load_paired_rows(pairs, src, first_column):
+            by_pair = src[0].bitcast(I32).rearrange("(u v i) w -> v i u w", u=2, i=LIVE)
+            columns = slice(first_column, first_column + src.shape[2])
+            for v in range(2):
+                nc.sync.dma_start(pairs[QUAD * v : QUAD * v + LIVE, :, columns].bitcast(I32), by_pair[v])
 
-        for i, src in enumerate((wb_scales, wc_scales)):
-            by_pair = src[0].bitcast(I32).rearrange("(u q r) c -> q r u c", u=2, r=4)
-            for q in range(2):
-                nc.sync.dma_start(wo_stage[32 * q : 32 * q + 4, :, i * N : (i + 1) * N].bitcast(I32), by_pair[q])
-        wb_w = sbt("wb_w", [P, N], U16)
-        nc.sync.dma_start(wb_w[:].bitcast(I32), wb_words[0].bitcast(I32))
-        wc_w = sbt("wc_w", [P, N], U32)
-        nc.sync.dma_start(wc_w[:].bitcast(I32), wc_words[0].rearrange("p n t -> p (n t)").bitcast(I32))
-        l6 = load_list("l6", offs6)
-        l3 = load_list("l3", offs3)
-        l4 = load_list("l4", offs4)
-        l5 = load_list("l5", offs5)
-        cols = {}
-        with nc.allow_non_contiguous_dma(reason="one value a partition"):
+        wt_plane = sb_tile("wt_plane", [P, V], U8)
+        xt_plane = sb_tile("xt_plane", [P, T], U8)
+        w2_plane = sb_tile("w2_plane", [P, R], U8)
+        out_pairs = sb_tile("out_pairs", [P, 2, 2 * N], U8)
+        out_plane = out_pairs[:, 0, :]
+        for zeroed in (w2_plane, wt_plane, out_pairs):
+            nc.vector.memset(zeroed[:].bitcast(I32), 0)
+
+        last_quad = QUADS - 1
+        w2_w = load_words(nc.gpsimd, "w2_w", fp8_rows(w2_words), R, U32)
+        xt_w = load_words(nc.sync, "xt_w", xt_words[0], T, U16)
+        for quad in range(last_quad):
+            load_filled_quadrant(nc.scalar, xt_plane, xt_scales, quad)
+        list2 = load_list("list2", offs2)
+        list1 = load_list("list1", offs)
+        load_filled_quadrant(nc.sync, xt_plane, xt_scales, last_quad)
+        wt_w = load_words(nc.sync, "wt_w", fp8_rows(wt_words), V, U32)
+        load_live_rows(nc.sync, w2_plane, w2_scales, range(QUADS))
+        load_live_rows(nc.sync, wt_plane, wt_scales, range(last_quad))
+        load_live_rows(nc.gpsimd, wt_plane, wt_scales, [last_quad])
+
+        load_paired_rows(out_pairs, wb_scales, 0)
+        load_paired_rows(out_pairs, wc_scales, N)
+        wb_w = load_words(nc.sync, "wb_w", wb_words[0], N, U16)
+        wc_w = load_words(nc.sync, "wc_w", fp8_rows(wc_words), N, U32)
+        list6 = load_list("list6", offs6)
+        list3 = load_list("list3", offs3)
+        list4 = load_list("list4", offs4)
+        list5 = load_list("list5", offs5)
+        per_feature = {}
+        with nc.allow_non_contiguous_dma(reason="one value a partition and group"):
             for name, src in (("sp2", sp2), ("bo2", bo2), ("so", so), ("sp", sp), ("bo", bo), ("so2", so2)):
-                col = sb.tile([P, 2, PAD], F32, name="col_" + name)
-                nc.sync.dma_start(col[:, :, 0:1], src.rearrange("(h p) o -> p h o", p=P))
-                cols[name] = col
+                values = sb.tile([P, GROUPS, PAD], F32, name="col_" + name)
+                nc.sync.dma_start(values[:, :, 0:1], src.rearrange("(g p) o -> p g o", p=P))
+                per_feature[name] = values
 
-        xg_w = sbt("xg_w", [P, J], U16)
-        nc.vector.tensor_copy(xg_w[:], xt_w[:].indirect(l2[:]))
-        xg_s = sbt("xg_s", [P, J], U8)
-        nc.vector.tensor_copy(xg_s[:], xt_s[:].indirect(l2[:]))
-        wg_w = sbt("wg_w", [P, R], U32)
-        nc.vector.tensor_copy(wg_w[:].rearrange("p (t m) -> p m t", t=PACK), wt_w[:].indirect(l1[:]))
-        wg_s = sbt("wg_s", [P, R], U8)
-        nc.vector.tensor_copy(wg_s[:].rearrange("p (t m) -> p m t", t=PACK), wt_s[:].indirect(l1[:]))
+        xg_w = sb_tile("xg_w", [P, J], U16)
+        nc.vector.tensor_copy(xg_w[:], xt_w[:].indirect(list2[:]))
+        xg_plane = sb_tile("xg_plane", [P, J], U8)
+        nc.vector.tensor_copy(xg_plane[:], xt_plane[:].indirect(list2[:]))
+        wg_w = sb_tile("wg_w", [P, R], U32)
+        nc.vector.tensor_copy(wg_w[:].rearrange("p (t m) -> p m t", t=PACK), wt_w[:].indirect(list1[:]))
+        wg_plane = sb_tile("wg_plane", [P, R], U8)
+        nc.vector.tensor_copy(wg_plane[:].rearrange("p (t m) -> p m t", t=PACK), wt_plane[:].indirect(list1[:]))
 
-        w2d_w = sbt("w2d_w", [P, R], U32)
+        w2d_w = sb_tile("w2d_w", [P, R], U32)
         nc.scalar.copy(w2d_w[:].rearrange("p (t m) -> p m t", t=PACK), w2_w[:].rearrange("p (m t) -> p m t", t=PACK))
-        w2d_s = sbt("w2d_s", [P, R], U8)
-        for t in range(PACK):
-            nc.gpsimd.tensor_copy(w2d_s[:, t * P : (t + 1) * P], w2_s[:, t::PACK])
+        w2d_plane = sb_tile("w2d_plane", [P, R], U8)
+        for t in range(0, PACK, DEAL):
+            nc.gpsimd.tensor_copy(
+                w2d_plane[:].rearrange("p (t m) -> p t m", t=PACK)[:, t : t + DEAL, :],
+                w2_plane[:].rearrange("p (m t) -> p t m", t=PACK)[:, t : t + DEAL, :],
+            )
 
-        def first_stage(bank, words, scales, fmt, h, t):
+        def first_stage(bank, words, plane, fmt, h, t):
             slots = slice(h * HALF, (h + 1) * HALF)
-            feats = slice(t * P, (t + 1) * P)
+            features = slice(t * P, (t + 1) * P)
             nc.tensor.matmul_mx(
                 out=bank[:, t, :],
-                lhsT=words[:, feats].bitcast(fmt),
-                lhsT_scale=scales[:, feats],
+                lhsT=words[:, features].bitcast(fmt),
+                lhsT_scale=plane[:, features],
                 rhs=xg_w[:, slots].bitcast(E2M1),
-                rhs_scale=xg_s[:, slots],
+                rhs_scale=xg_plane[:, slots],
                 start=True,
                 stop=True,
             )
 
-        b_banks = [psum.tile([P, PACK, HALF], F32, name="b_bank%d" % h) for h in range(2)]
-        a_banks = [psum.tile([P, PACK, HALF], F32, name="a_bank%d" % h) for h in range(2)]
-        for t in range(PACK):
-            for h in range(2):
-                first_stage(b_banks[h], w2d_w, w2d_s, E5M2, h, t)
-        b_sb = []
-        for h in range(2):
-            b_half = sbt("b_sb%d" % h, [P, HALF, PACK], F32)
-            nc.scalar.activation(b_half[:], b_banks[h][:].rearrange("p t j -> p j t"), ACT.Copy)
-            b_sb.append(b_half)
-        for h in range(2):
-            for t in range(PACK):
-                first_stage(a_banks[h], wg_w, wg_s, E4M3, h, t)
+        def by_slot(bank):
+            return bank[:].rearrange("p t j -> p j t")
 
-        for u in range(2):
-            nc.vector.tensor_copy(wo_s[64 * u : 64 * (u + 1), :].bitcast(I32), wo_stage[:, u, :].bitcast(I32))
+        b_banks = [psum.tile([P, PACK, HALF], F32, name="b_bank%d" % h, tag="b_bank%d" % h) for h in range(HALVES)]
+        a_banks = [psum.tile([P, PACK, HALF], F32, name="a_bank%d" % h) for h in range(HALVES)]
+        for t in range(PACK):
+            for h in range(HALVES):
+                first_stage(b_banks[h], w2d_w, w2d_plane, E5M2, h, t)
+        b_halves = []
+        for h in range(HALVES):
+            b_half = sb_tile("b_half%d" % h, [P, HALF, PACK], F32)
+            nc.scalar.activation(b_half[:], by_slot(b_banks[h]), ACT.Copy)
+            b_halves.append(b_half)
+        for h in range(HALVES):
+            for t in range(PACK):
+                first_stage(a_banks[h], wg_w, wg_plane, E4M3, h, t)
+
+        nc.vector.tensor_copy(out_pairs[P // 2 : P, 0, :].bitcast(I32), out_pairs[0 : P // 2, 1, :].bitcast(I32))
 
         hid = []
-        for h in range(2):
-            hid_half = sbt("hid%d" % h, [P, HALF, PACK], BF16)
-            for c in range(2):
-                part = slice(c * HALF // 2, (c + 1) * HALF // 2)
-                diff = sbt("diff%d%d" % (h, c), [P, HALF // 2, PACK], F32)
-                a_part = a_banks[h][:].rearrange("p t j -> p j t")[:, part, :]
-                nc.vector.tensor_tensor(diff[:], a_part, b_sb[h][:, part, :], ALU.subtract)
-                nc.scalar.activation(hid_half[:, part, :], diff[:], ACT.Abs)
+        for h in range(HALVES):
+            hid_half = sb_tile("hid%d" % h, [P, HALF, PACK], BF16)
+            for c in range(PARTS):
+                part = slice(c * PART, (c + 1) * PART)
+                is_last = h == HALVES - 1 and c == PARTS - 1
+                diff = sb_tile("diff%d%d" % (h, c), [P, PART, PACK], F32)
+                nc.vector.tensor_tensor(diff[:], by_slot(a_banks[h])[:, part, :], b_halves[h][:, part, :], ALU.subtract)
+                if is_last:
+                    nc.vector.scalar_tensor_tensor(hid_half[:, part, :], diff[:], -1.0, diff[:], ALU.mult, ALU.max)
+                else:
+                    nc.scalar.activation(hid_half[:, part, :], diff[:], ACT.Abs)
             hid.append(hid_half)
 
-        rows = {}
-        for which in ("p", "q"):
-            for g in range(2):
-                rows[which, g] = sbt("%s_rows%d" % (which, g), [P, J], F32)
-        second = {"p": (wb_w, E2M1, 0), "q": (wc_w, E5M2, N)}
-        order = [("p", 0), ("q", 0), ("p", 1), ("q", 1)]
-        for h in range(2):
-            hq_w = sbt("hq_w%d" % h, [P, HALF], U32)
-            hq_s = sbt("hq_s%d" % h, [P, HALF], U8)
-            nc.vector.quantize_mx(out=hq_w[:].bitcast(E5M2), scales=hq_s[:], in_=hid[h][:].rearrange("p j t -> p (j t)"))
-            if h == 0:
-                shared = psum.tile([P, 4, HALF], F32, name="o_bank0")
-                places = [shared[:, i, :] for i in range(4)]
-            else:
-                lone_p = psum.tile([P, HALF], F32, name="o_bank1")
-                lone_q = psum.tile([P, HALF], F32, name="o_bank2")
-                shared = psum.tile([P, 2, HALF], F32, name="o_bank3")
-                places = [lone_p[:], lone_q[:], shared[:, 0, :], shared[:, 1, :]]
-            for (which, g), place in zip(order, places):
-                words, fmt, s0 = second[which]
-                nc.tensor.matmul_mx(
-                    out=place,
-                    lhsT=words[:, g * P : (g + 1) * P].bitcast(fmt),
-                    lhsT_scale=wo_s[:, s0 + g * P : s0 + (g + 1) * P],
-                    rhs=hq_w[:].bitcast(E5M2),
-                    rhs_scale=hq_s[:],
-                    start=True,
-                    stop=True,
-                )
-            for key, place in zip(order, places):
-                nc.vector.tensor_copy(rows[key][:, h * HALF : (h + 1) * HALF], place)
+        p_rows = [sb_tile("p_rows%d" % g, [P, J], F32) for g in range(GROUPS)]
+        q_rows = [sb_tile("q_rows%d" % g, [P, J], F32) for g in range(GROUPS)]
+        hq_w = sb_tile("hq_w", [P, J], U32)
+        hq_plane = sb_tile("hq_plane", [P, J], U8)
 
-        for g in range(2):
-            def col(name):
-                return cols[name][:, g, 0:1]
+        def second_stage(sums, words, fmt, first_column, g, slots):
+            nc.tensor.matmul_mx(
+                out=sums,
+                lhsT=words[:, g * P : (g + 1) * P].bitcast(fmt),
+                lhsT_scale=out_plane[:, first_column + g * P : first_column + (g + 1) * P],
+                rhs=hq_w[:, slots].bitcast(E5M2),
+                rhs_scale=hq_plane[:, slots],
+                start=True,
+                stop=True,
+            )
 
-            p_rows, q_rows = rows["p", g], rows["q", g]
-            gate_q = sbt("gate_q%d" % g, [P, O], F32)
-            nc.scalar.activation(gate_q[:], p_rows[:].indirect(l6[:]), ACT.Sigmoid, bias=col("bo2"), scale=col("sp2"))
-            p_pick = sbt("p_pick%d" % g, [P, O], F32)
-            nc.scalar.activation(p_pick[:], p_rows[:].indirect(l3[:]), ACT.Copy, scale=col("so"))
-            gate_p = sbt("gate_p%d" % g, [P, O], F32)
-            nc.scalar.activation(gate_p[:], q_rows[:].indirect(l4[:]), ACT.Sigmoid, bias=col("bo"), scale=col("sp"))
-            q_pick = sbt("q_pick%d" % g, [P, O], F32)
-            nc.scalar.activation(q_pick[:], q_rows[:].indirect(l5[:]), ACT.Copy, scale=col("so2"))
-            first = sbt("first%d" % g, [P, O], F32)
-            nc.vector.tensor_tensor(first[:], p_pick[:], gate_p[:], ALU.mult)
-            other = sbt("other%d" % g, [P, O], F32)
-            nc.vector.tensor_tensor(other[:], q_pick[:], gate_q[:], ALU.mult)
-            result = sbt("result%d" % g, [P, O], F32)
-            nc.vector.tensor_tensor(result[:], first[:], other[:], ALU.subtract)
+        p_early = psum.tile([P, GROUPS, HALF], F32, name="p_early")
+        p_late = [psum.tile([P, HALF], F32, name="p_late%d" % g) for g in range(GROUPS)]
+        p_sums = [[p_early[:, g, :] for g in range(GROUPS)], [p_late[g][:] for g in range(GROUPS)]]
+        for h in range(HALVES):
+            slots = slice(h * HALF, (h + 1) * HALF)
+            nc.vector.quantize_mx(
+                out=hq_w[:, slots].bitcast(E5M2),
+                scales=hq_plane[:, slots],
+                in_=hid[h][:].rearrange("p j t -> p (j t)"),
+            )
+            for g in range(GROUPS):
+                second_stage(p_sums[h][g], wb_w, E2M1, 0, g, slots)
+            for g in range(GROUPS):
+                nc.vector.tensor_copy(p_rows[g][:, slots], p_sums[h][g])
+        for g in range(GROUPS):
+            q_bank = psum.tile([P, PACK, HALF], F32, name="q_bank%d" % g, tag="b_bank%d" % g)
+            q_sums = q_bank[:].rearrange("p t j -> p (t j)")[:, 0:J]
+            second_stage(q_sums, wc_w, E5M2, N, g, slice(0, J))
+            nc.vector.tensor_copy(q_rows[g][:], q_sums)
+
+        def look_up(name, windows, offsets, func, scale, bias=None):
+            results = []
+            for g in range(GROUPS):
+                picked = sb_tile("%s%d" % (name, g), [P, O], F32)
+                listed = windows[g][:].indirect(offsets[:])
+                scale_column = per_feature[scale][:, g, 0:1]
+                if bias is None:
+                    nc.scalar.activation(picked[:], listed, func, scale=scale_column)
+                else:
+                    nc.scalar.activation(picked[:], listed, func, bias=per_feature[bias][:, g, 0:1], scale=scale_column)
+                results.append(picked)
+            return results
+
+        gate_of_q = look_up("gate_of_q", p_rows, list6, ACT.Sigmoid, "sp2", "bo2")
+        p_scaled = look_up("p_scaled", p_rows, list3, ACT.Copy, "so")
+        gate_of_p = look_up("gate_of_p", q_rows, list4, ACT.Sigmoid, "sp", "bo")
+        q_scaled = look_up("q_scaled", q_rows, list5, ACT.Copy, "so2")
+
+        p_terms = []
+        for g in range(GROUPS):
+            p_term = sb_tile("p_term%d" % g, [P, O], F32)
+            nc.vector.tensor_tensor(p_term[:], p_scaled[g][:], gate_of_p[g][:], ALU.mult)
+            p_terms.append(p_term)
+        for g in range(GROUPS):
+            q_term = sb_tile("q_term%d" % g, [P, O], F32)
+            nc.vector.tensor_tensor(q_term[:], q_scaled[g][:], gate_of_q[g][:], ALU.mult)
+            result = sb_tile("result%d" % g, [P, O], F32)
+            nc.vector.tensor_tensor(result[:], p_terms[g][:], q_term[:], ALU.subtract)
             nc.sync.dma_start(out[g * P : (g + 1) * P, :], result[:])

from contextlib import ExitStack

import concourse.mybir as mybir

K, T, J, R, V, N, O = 512, 1024, 256, 512, 1024, 256, 128
FLOPS = 2 * (2 * K * R * J + 2 * R * N * J)

F32 = mybir.dt.float32
BF16 = mybir.dt.bfloat16
I32 = mybir.dt.int32
U32 = mybir.dt.uint32
U16 = mybir.dt.uint16
U8 = mybir.dt.uint8
E4M3 = mybir.dt.float8_e4m3fn_x4
E5M2 = mybir.dt.float8_e5m2_x4
E2M1 = mybir.dt.float4_e2m1fn_x4
ACT = mybir.ActivationFunctionType
ALU = mybir.AluOpType

P = 128
PACK = 4
QUADS = 4
QUAD = P // QUADS
LIVE = 4
HALVES = 2
HALF = J // HALVES
PARTS = 2
PART = HALF // PARTS
DEAL = 2
GROUPS = N // P
PAD = 8
ALIGN = 64


def tile_list_outcomegatedcross_storeleads_kernel(
    tc, xt_words, xt_scales, wt_words, wt_scales, w2_words, w2_scales, wb_words, wb_scales,
    wc_words, wc_scales, so, sp, bo, so2, sp2, bo2, offs, offs2, offs3, offs4, offs5, offs6, out,
):
    nc = tc.nc
    with ExitStack() as ctx:
        sb = ctx.enter_context(tc.tile_pool(name="sb", bufs=1))
        psum = ctx.enter_context(tc.psum_pool(name="psum", bufs=1))

        def sb_tile(name, shape, dtype):
            return sb.tile(shape, dtype, name=name, align_bytes=ALIGN)

        def load_list(name, src):
            offsets = sb.tile(list(src.shape), U16, name=name)
            nc.sync.dma_start(offsets[:], src)
            return offsets

        def load_words(queue, name, src, columns, dtype):
            words = sb_tile(name, [P, columns], dtype)
            queue.dma_start(words[:].bitcast(I32), src.bitcast(I32))
            return words

        def fp8_rows(src):
            return src[0].rearrange("p n t -> p (n t)")

        def load_live_rows(queue, plane, src, quadrants):
            for quad in quadrants:
                queue.dma_start(
                    plane[QUAD * quad : QUAD * quad + LIVE, :].bitcast(I32),
                    src[0, LIVE * quad : LIVE * (quad + 1), :].bitcast(I32),
                )

        def load_filled_quadrant(queue, plane, src, quad):
            rows = src[0, LIVE * quad : LIVE * (quad + 1), :].bitcast(I32)
            queue.dma_start(
                plane[QUAD * quad : QUAD * (quad + 1), :].bitcast(I32),
                rows.unsqueeze(0).broadcast_to([QUAD // LIVE, LIVE, rows.shape[1]]),
            )

        def load_paired_rows(pairs, src, first_column):
            by_pair = src[0].bitcast(I32).rearrange("(u v i) w -> v i u w", u=2, i=LIVE)
            columns = slice(first_column, first_column + src.shape[2])
            for v in range(2):
                nc.sync.dma_start(pairs[QUAD * v : QUAD * v + LIVE, :, columns].bitcast(I32), by_pair[v])

        wt_plane = sb_tile("wt_plane", [P, V], U8)
        xt_plane = sb_tile("xt_plane", [P, T], U8)
        w2_plane = sb_tile("w2_plane", [P, R], U8)
        out_pairs = sb_tile("out_pairs", [P, 2, 2 * N], U8)
        out_plane = out_pairs[:, 0, :]
        for zeroed in (w2_plane, wt_plane, out_pairs):
            nc.vector.memset(zeroed[:].bitcast(I32), 0)

        last_quad = QUADS - 1
        w2_w = load_words(nc.gpsimd, "w2_w", fp8_rows(w2_words), R, U32)
        xt_w = load_words(nc.sync, "xt_w", xt_words[0], T, U16)
        for quad in range(last_quad):
            load_filled_quadrant(nc.scalar, xt_plane, xt_scales, quad)
        list2 = load_list("list2", offs2)
        list1 = load_list("list1", offs)
        load_filled_quadrant(nc.sync, xt_plane, xt_scales, last_quad)
        wt_w = load_words(nc.sync, "wt_w", fp8_rows(wt_words), V, U32)
        load_live_rows(nc.sync, w2_plane, w2_scales, range(QUADS))
        load_live_rows(nc.sync, wt_plane, wt_scales, range(last_quad))
        load_live_rows(nc.gpsimd, wt_plane, wt_scales, [last_quad])

        load_paired_rows(out_pairs, wb_scales, 0)
        load_paired_rows(out_pairs, wc_scales, N)
        wb_w = load_words(nc.sync, "wb_w", wb_words[0], N, U16)
        wc_w = load_words(nc.sync, "wc_w", fp8_rows(wc_words), N, U32)
        list6 = load_list("list6", offs6)
        list3 = load_list("list3", offs3)
        list4 = load_list("list4", offs4)
        list5 = load_list("list5", offs5)
        per_feature = {}
        with nc.allow_non_contiguous_dma(reason="one value a partition and group"):
            for name, src in (("sp2", sp2), ("bo2", bo2), ("so", so), ("sp", sp), ("bo", bo), ("so2", so2)):
                values = sb.tile([P, GROUPS, PAD], F32, name="col_" + name)
                nc.sync.dma_start(values[:, :, 0:1], src.rearrange("(g p) o -> p g o", p=P))
                per_feature[name] = values

        xg_w = sb_tile("xg_w", [P, J], U16)
        nc.vector.tensor_copy(xg_w[:], xt_w[:].indirect(list2[:]))
        xg_plane = sb_tile("xg_plane", [P, J], U8)
        nc.vector.tensor_copy(xg_plane[:], xt_plane[:].indirect(list2[:]))
        wg_w = sb_tile("wg_w", [P, R], U32)
        nc.vector.tensor_copy(wg_w[:].rearrange("p (t m) -> p m t", t=PACK), wt_w[:].indirect(list1[:]))
        wg_plane = sb_tile("wg_plane", [P, R], U8)
        nc.vector.tensor_copy(wg_plane[:].rearrange("p (t m) -> p m t", t=PACK), wt_plane[:].indirect(list1[:]))

        w2d_w = sb_tile("w2d_w", [P, R], U32)
        nc.scalar.copy(w2d_w[:].rearrange("p (t m) -> p m t", t=PACK), w2_w[:].rearrange("p (m t) -> p m t", t=PACK))
        w2d_plane = sb_tile("w2d_plane", [P, R], U8)
        for t in range(0, PACK, DEAL):
            nc.gpsimd.tensor_copy(
                w2d_plane[:].rearrange("p (t m) -> p t m", t=PACK)[:, t : t + DEAL, :],
                w2_plane[:].rearrange("p (m t) -> p t m", t=PACK)[:, t : t + DEAL, :],
            )

        def first_stage(bank, words, plane, fmt, h, t):
            slots = slice(h * HALF, (h + 1) * HALF)
            features = slice(t * P, (t + 1) * P)
            nc.tensor.matmul_mx(
                out=bank[:, t, :],
                lhsT=words[:, features].bitcast(fmt),
                lhsT_scale=plane[:, features],
                rhs=xg_w[:, slots].bitcast(E2M1),
                rhs_scale=xg_plane[:, slots],
                start=True,
                stop=True,
            )

        def by_slot(bank):
            return bank[:].rearrange("p t j -> p j t")

        b_banks = [psum.tile([P, PACK, HALF], F32, name="b_bank%d" % h, tag="b_bank%d" % h) for h in range(HALVES)]
        a_banks = [psum.tile([P, PACK, HALF], F32, name="a_bank%d" % h) for h in range(HALVES)]
        for t in range(PACK):
            for h in range(HALVES):
                first_stage(b_banks[h], w2d_w, w2d_plane, E5M2, h, t)
        b_halves = []
        for h in range(HALVES):
            b_half = sb_tile("b_half%d" % h, [P, HALF, PACK], F32)
            nc.scalar.activation(b_half[:], by_slot(b_banks[h]), ACT.Copy)
            b_halves.append(b_half)
        for h in range(HALVES):
            for t in range(PACK):
                first_stage(a_banks[h], wg_w, wg_plane, E4M3, h, t)

        nc.vector.tensor_copy(out_pairs[P // 2 : P, 0, :].bitcast(I32), out_pairs[0 : P // 2, 1, :].bitcast(I32))

        hid = []
        for h in range(HALVES):
            hid_half = sb_tile("hid%d" % h, [P, HALF, PACK], BF16)
            for c in range(PARTS):
                part = slice(c * PART, (c + 1) * PART)
                is_last = h == HALVES - 1 and c == PARTS - 1
                diff = sb_tile("diff%d%d" % (h, c), [P, PART, PACK], F32)
                nc.vector.tensor_tensor(diff[:], by_slot(a_banks[h])[:, part, :], b_halves[h][:, part, :], ALU.subtract)
                if is_last:
                    nc.vector.scalar_tensor_tensor(hid_half[:, part, :], diff[:], -1.0, diff[:], ALU.mult, ALU.max)
                else:
                    nc.scalar.activation(hid_half[:, part, :], diff[:], ACT.Abs)
            hid.append(hid_half)

        p_rows = [sb_tile("p_rows%d" % g, [P, J], F32) for g in range(GROUPS)]
        q_rows = [sb_tile("q_rows%d" % g, [P, J], F32) for g in range(GROUPS)]
        hq_w = sb_tile("hq_w", [P, J], U32)
        hq_plane = sb_tile("hq_plane", [P, J], U8)

        def second_stage(sums, words, fmt, first_column, g, slots):
            nc.tensor.matmul_mx(
                out=sums,
                lhsT=words[:, g * P : (g + 1) * P].bitcast(fmt),
                lhsT_scale=out_plane[:, first_column + g * P : first_column + (g + 1) * P],
                rhs=hq_w[:, slots].bitcast(E5M2),
                rhs_scale=hq_plane[:, slots],
                start=True,
                stop=True,
            )

        p_early = psum.tile([P, GROUPS, HALF], F32, name="p_early")
        p_late = [psum.tile([P, HALF], F32, name="p_late%d" % g) for g in range(GROUPS)]
        p_sums = [[p_early[:, g, :] for g in range(GROUPS)], [p_late[g][:] for g in range(GROUPS)]]
        for h in range(HALVES):
            slots = slice(h * HALF, (h + 1) * HALF)
            nc.vector.quantize_mx(
                out=hq_w[:, slots].bitcast(E5M2),
                scales=hq_plane[:, slots],
                in_=hid[h][:].rearrange("p j t -> p (j t)"),
            )
            for g in range(GROUPS):
                second_stage(p_sums[h][g], wb_w, E2M1, 0, g, slots)
            for g in range(GROUPS):
                nc.vector.tensor_copy(p_rows[g][:, slots], p_sums[h][g])
        for g in range(GROUPS):
            q_bank = psum.tile([P, PACK, HALF], F32, name="q_bank%d" % g, tag="b_bank%d" % g)
            q_sums = q_bank[:].rearrange("p t j -> p (t j)")[:, 0:J]
            second_stage(q_sums, wc_w, E5M2, N, g, slice(0, J))
            nc.vector.tensor_copy(q_rows[g][:], q_sums)

        def look_up(name, windows, offsets, func, scale, bias=None):
            results = []
            for g in range(GROUPS):
                picked = sb_tile("%s%d" % (name, g), [P, O], F32)
                listed = windows[g][:].indirect(offsets[:])
                scale_column = per_feature[scale][:, g, 0:1]
                if bias is None:
                    nc.scalar.activation(picked[:], listed, func, scale=scale_column)
                else:
                    nc.scalar.activation(picked[:], listed, func, bias=per_feature[bias][:, g, 0:1], scale=scale_column)
                results.append(picked)
            return results

        gate_of_q = look_up("gate_of_q", p_rows, list6, ACT.Sigmoid, "sp2", "bo2")
        p_scaled = look_up("p_scaled", p_rows, list3, ACT.Copy, "so")
        gate_of_p = look_up("gate_of_p", q_rows, list4, ACT.Sigmoid, "sp", "bo")
        q_scaled = look_up("q_scaled", q_rows, list5, ACT.Copy, "so2")

        p_terms = []
        for g in range(GROUPS):
            p_term = sb_tile("p_term%d" % g, [P, O], F32)
            nc.vector.tensor_tensor(p_term[:], p_scaled[g][:], gate_of_p[g][:], ALU.mult)
            p_terms.append(p_term)
        for g in range(GROUPS):
            q_term = sb_tile("q_term%d" % g, [P, O], F32)
            nc.vector.tensor_tensor(q_term[:], q_scaled[g][:], gate_of_q[g][:], ALU.mult)
            result = sb_tile("result%d" % g, [P, O], F32)
            nc.vector.tensor_tensor(result[:], p_terms[g][:], q_term[:], ALU.subtract)
            nc.sync.dma_start(out[g * P : (g + 1) * P, :], result[:])
